import numpy as np
import ml_dtypes


def mxq(x, axis, fmt="e4m3"):
    dtype, down = {"e4m3": (ml_dtypes.float8_e4m3fn, 7), "e5m2": (ml_dtypes.float8_e5m2, 14)}[fmt]
    v = np.moveaxis(np.asarray(x, np.float32).astype(ml_dtypes.bfloat16).astype(np.float64), axis, -1)
    blocks = v.reshape(v.shape[:-1] + (-1, 32))
    amax = np.abs(blocks).max(-1, keepdims=True)
    byte = np.maximum(np.where(amax > 0, np.frexp(amax)[1] - 1 + 127, 0) - down, 1)
    scale = np.exp2(byte - 127.0)
    codes = (blocks / scale).astype(np.float32).astype(dtype).astype(np.float64)
    return np.moveaxis((codes * scale).reshape(v.shape), -1, axis)


WIDE = False


def mx_kscale(k):
    if not WIDE:
        return np.ones(k)
    levels = np.array([30, -30])
    if k % 512:
        return np.exp2(np.random.permutation(np.resize(levels, k // 32))).repeat(32)
    a = np.empty((k // 512, 16))
    for p in range(k // 512):
        a[p, :8] = np.random.permutation(np.resize(levels, 8))
        for g in range(8):
            far = levels[np.abs(levels - a[p, g]) >= 10]
            a[p, g + 8] = far[np.random.randint(len(far))]
    return np.exp2(a.ravel()).repeat(32)


BF16 = ml_dtypes.bfloat16


def bf(x):
    return np.asarray(x, np.float32).astype(BF16)


def f64(x):
    return np.asarray(x).astype(np.float64)


E2M1 = np.array([0.0, 0.5, 1.0, 1.5, 2.0, 3.0, 4.0, 6.0, -0.0, -0.5, -1.0, -1.5, -2.0, -3.0, -4.0, -6.0])


def pack_weight(w, fmt):
    k, n = w.shape
    w = f64(bf(w)).reshape(k // 32, 32, n)
    amax = np.abs(w).max(1)
    if fmt in ("e4m3", "e5m2"):
        byte = np.frexp(amax)[1] - 1 + 127 - (7 if fmt == "e4m3" else 14)
    else:
        mant, ex = np.frexp(amax / 6.0)
        byte = np.where(mant > 0.5, ex, ex - 1) + 127
    byte = np.clip(np.where(amax > 0, byte, 1), 1, 254)
    scaled = (w * np.exp2(127.0 - byte)[:, None, :]).reshape(k, n).astype(np.float32)
    by_word = np.ascontiguousarray(scaled.reshape(k // 512, 128, 4, n).transpose(0, 1, 3, 2))
    if fmt in ("e4m3", "e5m2"):
        words = by_word.astype(ml_dtypes.float8_e4m3fn if fmt == "e4m3" else ml_dtypes.float8_e5m2).view(np.uint8)
    else:
        c = by_word.astype(ml_dtypes.float4_e2m1fn).view(np.uint8) & 0xF
        words = c[..., 0::2] | (c[..., 1::2] << 4)
    return np.ascontiguousarray(words), np.ascontiguousarray(byte.astype(np.uint8).reshape(k // 512, 16, n))


def unpack_weight(words, scales, fmt):
    g, p, n, _ = words.shape
    if fmt in ("e4m3", "e5m2"):
        vals = np.ascontiguousarray(words).view(ml_dtypes.float8_e4m3fn if fmt == "e4m3" else ml_dtypes.float8_e5m2).astype(np.float64)
    else:
        nib = np.empty((g, p, n, 4), np.uint8)
        nib[..., 0::2] = words & 0xF
        nib[..., 1::2] = words >> 4
        vals = E2M1[nib]
    vals = vals * np.repeat(np.exp2(scales.astype(np.float64) - 127.0), 8, axis=1)[..., None]
    return vals.transpose(0, 1, 3, 2).reshape(g * 512, n)


R, B, C = 1024, 1024, 2048


def setup_inputs():
    s = mx_kscale(B)
    t = mx_kscale(B)
    E = np.random.standard_normal((B, R)) * np.exp(0.5 * np.random.standard_normal((B, R)))
    e_words, e_scales = pack_weight(E * s[:, None], "e5m2")
    return {"e_words": e_words,
            "e_scales": e_scales,
            "u_rows": bf(np.random.standard_normal((B, C)) / np.sqrt(B) / s[:, None]),
            "w_block": bf(np.random.standard_normal((R, B)) * t),
            "asym_rows": bf(np.random.standard_normal((B, C)) / np.sqrt(B) / t[:, None]),
            "w_rest": bf(np.random.standard_normal((R, C))),
            "inv_step": bf(1 + 0.1 * np.random.standard_normal(R)),
            "offset": bf(0.3 * np.random.standard_normal(R))}


def reference(e_words, e_scales, u_rows, w_block, asym_rows, w_rest, inv_step, offset):
    E = unpack_weight(e_words, e_scales, "e5m2")
    U = mxq(f64(u_rows), 0, "e4m3")
    V = mxq(f64(w_block), 1, "e4m3")
    A = mxq(f64(asym_rows), 0, "e4m3")
    delta = (E.T @ U) + (V @ A)
    updated = f64(w_rest) + delta
    return updated * f64(inv_step)[:, None] + f64(offset)[:, None]

@@ -1,0 +1,280 @@
+from contextlib import ExitStack
+
+import concourse.mybir as mybir
+from concourse.masks import make_identity
+
+R, B, C = 1024, 1024, 2048
+FLOPS = 2 * 2 * R * B * C
+
+F32 = mybir.dt.float32
+BF16 = mybir.dt.bfloat16
+I32 = mybir.dt.int32
+U32 = mybir.dt.uint32
+U8 = mybir.dt.uint8
+E4M3X4 = mybir.dt.float8_e4m3fn_x4
+E5M2X4 = mybir.dt.float8_e5m2_x4
+IDENTITY = mybir.ActivationFunctionType.Identity
+MULT = mybir.AluOpType.mult
+ADD = mybir.AluOpType.add
+
+P = 128
+PACK = 4
+K_PASS = P * PACK
+PASSES = B // K_PASS
+N_TILE = 512
+ROW_TILES = R // P
+CHUNKS = C // N_TILE
+HALF = ROW_TILES // 2
+VECTOR_COLUMNS = (288, 288, 256, 256)
+LAG = 6
+STORE_RUNS = ((4, 4), (4, 4), (4, 4), (4, 2, 1, 1))
+
+
+def tile_block_error_column_update_e4_kernel(
+    tc, e_words, e_scales, u_rows, w_block, asym_rows, w_rest, inv_step, offset, out
+):
+    nc = tc.nc
+    with ExitStack() as ctx:
+        keep = ctx.enter_context(tc.tile_pool(name="keep", bufs=1))
+        stage = ctx.enter_context(tc.tile_pool(name="stage", bufs=5))
+        psum = ctx.enter_context(tc.psum_pool(name="psum", bufs=1))
+        ctx.enter_context(tc.manual_schedule())
+
+        slabs = [(asym_rows, 0), (asym_rows, 1), (u_rows, 0), (u_rows, 1)]
+        slab_raw, slab_grouped, slab_mx = {}, {}, {}
+        v_raw, v_grouped, v_mx = {}, {}, {}
+        e_codes, w_raw, acc, result = {}, {}, {}, {}
+
+        def bank(b):
+            return psum.tile([P, N_TILE], F32, name="bank%d" % b)
+
+        def load_slab(j, s, slot):
+            source, g = slabs[s]
+            raw = keep.tile([P, PACK, N_TILE], BF16, name="raw%d" % slot)
+            rows = source[g * K_PASS : (g + 1) * K_PASS, j * N_TILE : (j + 1) * N_TILE]
+            nc.sync.dma_start(out=raw[:], in_=rows.rearrange("(p t) c -> p t c", t=PACK))
+            slab_raw[j, s] = raw
+
+        def load_v(pair):
+            raw = keep.tile([P, 2, B], BF16, name="raw%d" % (8 + pair))
+            rows = w_block[pair * 2 * P : (pair + 1) * 2 * P, :]
+            nc.sync.dma_start(out=raw[:], in_=rows.rearrange("(i m) k -> m i k", m=P))
+            v_raw[pair] = raw
+
+        def load_e(half):
+            width = HALF * P
+            codes = keep.tile([P, PASSES, width], U32, name="e_codes%d" % half, align_bytes=64)
+            words = e_words.rearrange("g p n t -> p g (n t)")
+            words = words[:, :, half * width * PACK : (half + 1) * width * PACK]
+            nc.sync.dma_start(out=codes[:].bitcast(I32), in_=words.bitcast(I32))
+            e_codes[half] = codes
+
+        def load_w(j, first, count):
+            raw = keep.tile([P, count, N_TILE], BF16, name="w%d_%d" % (j, first))
+            rows = w_rest[first * P : (first + count) * P, j * N_TILE : (j + 1) * N_TILE]
+            nc.sync.dma_start(out=raw[:], in_=rows.rearrange("(i m) c -> m i c", m=P))
+            for i in range(count):
+                w_raw[j * ROW_TILES + first + i] = raw[:, i, :]
+
+        def interleave(j, s):
+            grouped = stage.tile([P, N_TILE, PACK], BF16, name="grouped", align_bytes=64)
+            split = VECTOR_COLUMNS[j]
+            raw = slab_raw[j, s]
+            nc.vector.tensor_copy(
+                out=grouped[:, :split, :].rearrange("p (c i) t -> p c t i", i=4),
+                in_=raw[:, :, :split].rearrange("p t (c i) -> p c t i", i=4),
+            )
+            nc.scalar.copy(
+                out=grouped[:, split:, :].rearrange("p (c i) t -> p c t i", i=4),
+                in_=raw[:, :, split:].rearrange("p t (c i) -> p c t i", i=4),
+            )
+            slab_grouped[j, s] = grouped
+
+        def quantize(grouped, name):
+            codes = keep.tile([P, N_TILE], U32, name="codes_" + name, align_bytes=64)
+            scales = keep.tile([P, N_TILE], U8, name="scales_" + name, align_bytes=64)
+            nc.vector.quantize_mx(out=codes[:].bitcast(E4M3X4), scales=scales[:], in_=grouped)
+            return codes, scales
+
+        def quantize_slab(j, s):
+            slab_mx[j, s] = quantize(slab_grouped[j, s][:].rearrange("p c t -> p (c t)"), "%d_%d" % (j, s))
+
+        def quantize_v(pair):
+            v_mx[pair] = quantize(v_grouped[pair][:], "v%d" % pair)
+
+        def turn_v(pair):
+            grouped = stage.tile([P, N_TILE * PACK], BF16, name="grouped", align_bytes=64)
+            for i in range(2):
+                words = v_raw[pair][:, i, :].bitcast(F32)
+                turned = bank(HALF + (2 * pair + i) % HALF)
+                for g in range(PASSES):
+                    for u in range(2):
+                        slot = (2 * g + u) * P
+                        nc.tensor.transpose(
+                            turned[:, slot : slot + P], words[:, 2 * P * g + u : 2 * P * (g + 1) : 2], identity[:]
+                        )
+                nc.scalar.copy(
+                    out=grouped[:, i * B : (i + 1) * B].bitcast(F32).rearrange("p (g m u) -> p g m u", g=PASSES, u=2),
+                    in_=turned[:].rearrange("p (g u m) -> p g m u", g=PASSES, u=2),
+                )
+            v_grouped[pair] = grouped
+
+        def multiply(n, s):
+            j, i = divmod(n, ROW_TILES)
+            g = slabs[s][1]
+            if s == 0:
+                acc[n] = bank(i)
+            if s < PASSES:
+                codes, scales = v_mx[i // 2]
+                cols = slice((i % 2 * PASSES + g) * P, (i % 2 * PASSES + g + 1) * P)
+                lhs, lhs_scale = codes[:, cols].bitcast(E4M3X4), scales[:, cols]
+            else:
+                lhs = e_codes[i // HALF][:, g, i % HALF * P : (i % HALF + 1) * P].bitcast(E5M2X4)
+                lhs_scale = e_plane[:, g, i * P : (i + 1) * P]
+            rhs_codes, rhs_scales = slab_mx[j, s]
+            nc.tensor.matmul_mx(
+                out=acc[n][:],
+                lhsT=lhs,
+                lhsT_scale=lhs_scale,
+                rhs=rhs_codes[:].bitcast(E4M3X4),
+                rhs_scale=rhs_scales[:],
+                start=(s == 0),
+                stop=(s == len(slabs) - 1),
+            )
+
+        def multiply_tile(n):
+            for s in range(len(slabs)):
+                multiply(n, s)
+
+        runs = {}
+        for j in range(CHUNKS):
+            first = 0
+            for count in STORE_RUNS[j]:
+                staged = keep.tile([P, count, N_TILE], F32, name="out%d_%d" % (j, first))
+                for i in range(count):
+                    result[j * ROW_TILES + first + i] = staged[:, i, :]
+                runs[j * ROW_TILES + first + count - 1] = (staged, j, first, count)
+                first = first + count
+
+        def scale_w(n):
+            i = n % ROW_TILES
+            nc.scalar.activation(
+                out=result[n],
+                in_=w_raw[n],
+                func=IDENTITY,
+                scale=by_row[:, i : i + 1],
+                bias=by_row[:, ROW_TILES + i : ROW_TILES + i + 1],
+            )
+
+        def finish(n):
+            i = n % ROW_TILES
+            nc.vector.scalar_tensor_tensor(
+                out=result[n], in0=acc[n][:], scalar=by_row[:, i : i + 1], in1=result[n], op0=MULT, op1=ADD
+            )
+            if n in runs:
+                staged, j, first, count = runs[n]
+                rows = out[first * P : (first + count) * P, j * N_TILE : (j + 1) * N_TILE]
+                nc.sync.dma_start(out=rows.rearrange("(i m) c -> m i c", m=P), in_=staged[:])
+
+        vec_rows = keep.tile([2 * ROW_TILES, P], BF16)
+        nc.gpsimd.dma_start(out=vec_rows[:ROW_TILES, :], in_=inv_step.rearrange("(i m) -> i m", m=P))
+        nc.gpsimd.dma_start(out=vec_rows[ROW_TILES:, :], in_=offset.rearrange("(i m) -> i m", m=P))
+        identity = keep.tile([P, P], F32)
+        make_identity(nc, identity[:])
+        vec_square = keep.tile([P, P], F32)
+        nc.gpsimd.memset(vec_square[:], 0.0)
+        e_plane = keep.tile([P, PASSES, R], U8, align_bytes=64)
+        nc.vector.memset(e_plane[:].bitcast(I32), 0)
+
+        load_v(0)
+        load_slab(0, 0, 0)
+        load_slab(0, 1, 1)
+        load_v(1)
+        for q in range(4):
+            nc.sync.dma_start(
+                out=e_plane[32 * q : 32 * q + 4, :, :].bitcast(I32),
+                in_=e_scales[:, 4 * q : 4 * q + 4, :].rearrange("g r n -> r g n").bitcast(I32),
+            )
+        load_slab(0, 2, 2)
+        load_slab(0, 3, 3)
+        load_e(0)
+        load_v(2)
+        load_v(3)
+        load_e(1)
+        for s in range(len(slabs)):
+            load_slab(1, s, 4 + s)
+        load_w(0, 0, HALF)
+        load_w(0, HALF, HALF)
+
+        nc.scalar.activation(out=vec_square[: 2 * ROW_TILES, :], in_=vec_rows[:], func=IDENTITY)
+        turn_v(0)
+        interleave(0, 0)
+        interleave(0, 1)
+        quantize_v(0)
+        quantize_slab(0, 0)
+        turn_v(1)
+        vec_turned = bank(HALF)
+        nc.tensor.transpose(vec_turned[:, :P], vec_square[:], identity[:])
+        by_row = keep.tile([P, 2 * ROW_TILES], F32)
+        nc.scalar.copy(out=by_row[:], in_=vec_turned[:, : 2 * ROW_TILES])
+        interleave(0, 2)
+        quantize_slab(0, 1)
+        quantize_v(1)
+        interleave(0, 3)
+        quantize_slab(0, 2)
+        quantize_slab(0, 3)
+        for n in range(HALF):
+            multiply(n, 0)
+            multiply(n, 1)
+        for s in (2, 3):
+            for n in range(HALF):
+                multiply(n, s)
+
+        turn_v(2)
+        turn_v(3)
+        for s in range(len(slabs)):
+            load_slab(2, s, s)
+        load_w(1, 0, ROW_TILES)
+        for s in range(len(slabs)):
+            load_slab(3, s, 8 + s)
+        load_w(2, 0, ROW_TILES)
+        load_w(3, 0, ROW_TILES)
+
+        interleave(1, 0)
+        quantize_v(2)
+        interleave(1, 1)
+        quantize_v(3)
+        for n in range(HALF, ROW_TILES):
+            multiply_tile(n)
+        quantize_slab(1, 0)
+        interleave(1, 2)
+        quantize_slab(1, 1)
+        scale_w(0)
+        interleave(1, 3)
+        scale_w(1)
+        scale_w(2)
+        quantize_slab(1, 2)
+        finish(0)
+        quantize_slab(1, 3)
+        finish(1)
+
+        for n in range(ROW_TILES, (CHUNKS - 1) * ROW_TILES):
+            j, i = divmod(n, ROW_TILES)
+            multiply_tile(n)
+            if i % 2 == 0:
+                interleave(j + 1, i // 2)
+            scale_w(n - LAG + 1)
+            finish(n - LAG)
+            if i % 2 == 1:
+                quantize_slab(j + 1, i // 2)
+
+        done = (CHUNKS - 1) * ROW_TILES - LAG
+        last = CHUNKS * ROW_TILES
+        for n in range((CHUNKS - 1) * ROW_TILES, last):
+            multiply_tile(n)
+            upto = min(done + 2, n + 1)
+            for m in range(done, upto):
+                if m + 1 < last:
+                    scale_w(m + 1)
+                finish(m)
+            done = upto

@@ -25,9 +25,8 @@ N_TILE = 512
 ROW_TILES = R // P
 CHUNKS = C // N_TILE
 HALF = ROW_TILES // 2
-VECTOR_COLUMNS = (288, 288, 256, 256)
-LAG = 6
-STORE_RUNS = ((4, 4), (4, 4), (4, 4), (4, 2, 1, 1))
+VECTOR_COLUMNS = (288, 256)
+STORES = ((0, 2, (2, 2, 2, 2)), (2, 1, (4, 4)), (3, 1, (4, 2, 1, 1)))
 
 
 def tile_block_error_column_update_e4_kernel(
@@ -42,21 +41,25 @@ def tile_block_error_column_update_e4_kernel(
 
         slabs = [(asym_rows, 0), (asym_rows, 1), (u_rows, 0), (u_rows, 1)]
         slab_raw, slab_grouped, slab_mx = {}, {}, {}
-        v_raw, v_grouped, v_mx = {}, {}, {}
+        v_raw, v_turned, v_grouped, v_mx = {}, {}, {}, {}
         e_codes, w_raw, acc, result = {}, {}, {}, {}
+
+        tiles = [(j, half * HALF + i) for half in range(2) for j in range(2) for i in range(HALF)]
+        tiles = tiles + [(j, i) for j in range(2, CHUNKS) for i in range(ROW_TILES)]
 
         def bank(b):
             return psum.tile([P, N_TILE], F32, name="bank%d" % b)
 
-        def load_slab(j, s, slot):
+        def load_slab(j, s):
             source, g = slabs[s]
-            raw = keep.tile([P, PACK, N_TILE], BF16, name="raw%d" % slot)
-            rows = source[g * K_PASS : (g + 1) * K_PASS, j * N_TILE : (j + 1) * N_TILE]
+            raw = keep.tile([P, PACK, 2 * N_TILE], BF16, name="raw%d" % s)
+            rows = source[g * K_PASS : (g + 1) * K_PASS, j * N_TILE : (j + 2) * N_TILE]
             nc.sync.dma_start(out=raw[:], in_=rows.rearrange("(p t) c -> p t c", t=PACK))
-            slab_raw[j, s] = raw
+            for d in range(2):
+                slab_raw[j + d, s] = raw[:, :, d * N_TILE : (d + 1) * N_TILE]
 
         def load_v(pair):
-            raw = keep.tile([P, 2, B], BF16, name="raw%d" % (8 + pair))
+            raw = keep.tile([P, 2, B], BF16, name="v_raw%d" % pair)
             rows = w_block[pair * 2 * P : (pair + 1) * 2 * P, :]
             nc.sync.dma_start(out=raw[:], in_=rows.rearrange("(i m) k -> m i k", m=P))
             v_raw[pair] = raw
@@ -69,16 +72,17 @@ def tile_block_error_column_update_e4_kernel(
             nc.sync.dma_start(out=codes[:].bitcast(I32), in_=words.bitcast(I32))
             e_codes[half] = codes
 
-        def load_w(j, first, count):
-            raw = keep.tile([P, count, N_TILE], BF16, name="w%d_%d" % (j, first))
-            rows = w_rest[first * P : (first + count) * P, j * N_TILE : (j + 1) * N_TILE]
+        def load_w(j, half):
+            raw = keep.tile([P, HALF, 2 * N_TILE], BF16, name="w%d_%d" % (j, half))
+            rows = w_rest[half * HALF * P : (half + 1) * HALF * P, j * N_TILE : (j + 2) * N_TILE]
             nc.sync.dma_start(out=raw[:], in_=rows.rearrange("(i m) c -> m i c", m=P))
-            for i in range(count):
-                w_raw[j * ROW_TILES + first + i] = raw[:, i, :]
+            for i in range(HALF):
+                for d in range(2):
+                    w_raw[j + d, half * HALF + i] = raw[:, i, d * N_TILE : (d + 1) * N_TILE]
 
         def interleave(j, s):
             grouped = stage.tile([P, N_TILE, PACK], BF16, name="grouped", align_bytes=64)
-            split = VECTOR_COLUMNS[j]
+            split = VECTOR_COLUMNS[j // 2]
             raw = slab_raw[j, s]
             nc.vector.tensor_copy(
                 out=grouped[:, :split, :].rearrange("p (c i) t -> p c t i", i=4),
@@ -103,7 +107,6 @@ def tile_block_error_column_update_e4_kernel(
             v_mx[pair] = quantize(v_grouped[pair][:], "v%d" % pair)
 
         def turn_v(pair):
-            grouped = stage.tile([P, N_TILE * PACK], BF16, name="grouped", align_bytes=64)
             for i in range(2):
                 words = v_raw[pair][:, i, :].bitcast(F32)
                 turned = bank(HALF + (2 * pair + i) % HALF)
@@ -113,6 +116,12 @@ def tile_block_error_column_update_e4_kernel(
                         nc.tensor.transpose(
                             turned[:, slot : slot + P], words[:, 2 * P * g + u : 2 * P * (g + 1) : 2], identity[:]
                         )
+                v_turned[2 * pair + i] = turned
+
+        def group_v(pair):
+            grouped = stage.tile([P, N_TILE * PACK], BF16, name="grouped", align_bytes=64)
+            for i in range(2):
+                turned = v_turned[2 * pair + i]
                 nc.scalar.copy(
                     out=grouped[:, i * B : (i + 1) * B].bitcast(F32).rearrange("p (g m u) -> p g m u", g=PASSES, u=2),
                     in_=turned[:].rearrange("p (g u m) -> p g m u", g=PASSES, u=2),
@@ -120,10 +129,10 @@ def tile_block_error_column_update_e4_kernel(
             v_grouped[pair] = grouped
 
         def multiply(n, s):
-            j, i = divmod(n, ROW_TILES)
+            j, i = tiles[n]
             g = slabs[s][1]
             if s == 0:
-                acc[n] = bank(i)
+                acc[n] = bank(n % ROW_TILES)
             if s < PASSES:
                 codes, scales = v_mx[i // 2]
                 cols = slice((i % 2 * PASSES + g) * P, (i % 2 * PASSES + g + 1) * P)
@@ -147,128 +156,163 @@ def tile_block_error_column_update_e4_kernel(
                 multiply(n, s)
 
         runs = {}
-        for j in range(CHUNKS):
+        for j, span, counts in STORES:
             first = 0
-            for count in STORE_RUNS[j]:
-                staged = keep.tile([P, count, N_TILE], F32, name="out%d_%d" % (j, first))
+            for count in counts:
+                staged = keep.tile([P, count, span * N_TILE], F32, name="out%d_%d" % (j, first))
                 for i in range(count):
-                    result[j * ROW_TILES + first + i] = staged[:, i, :]
-                runs[j * ROW_TILES + first + count - 1] = (staged, j, first, count)
+                    for d in range(span):
+                        result[j + d, first + i] = staged[:, i, d * N_TILE : (d + 1) * N_TILE]
+                rows = out[first * P : (first + count) * P, j * N_TILE : (j + span) * N_TILE]
+                runs[j + span - 1, first + count - 1] = (staged, rows)
                 first = first + count
 
         def scale_w(n):
-            i = n % ROW_TILES
+            i = tiles[n][1]
             nc.scalar.activation(
-                out=result[n],
-                in_=w_raw[n],
+                out=result[tiles[n]],
+                in_=w_raw[tiles[n]],
                 func=IDENTITY,
                 scale=by_row[:, i : i + 1],
                 bias=by_row[:, ROW_TILES + i : ROW_TILES + i + 1],
             )
 
         def finish(n):
-            i = n % ROW_TILES
+            i = tiles[n][1]
+            target = result[tiles[n]]
             nc.vector.scalar_tensor_tensor(
-                out=result[n], in0=acc[n][:], scalar=by_row[:, i : i + 1], in1=result[n], op0=MULT, op1=ADD
+                out=target, in0=acc[n][:], scalar=by_row[:, i : i + 1], in1=target, op0=MULT, op1=ADD
             )
-            if n in runs:
-                staged, j, first, count = runs[n]
-                rows = out[first * P : (first + count) * P, j * N_TILE : (j + 1) * N_TILE]
+            if tiles[n] in runs:
+                staged, rows = runs[tiles[n]]
                 nc.sync.dma_start(out=rows.rearrange("(i m) c -> m i c", m=P), in_=staged[:])
 
         vec_rows = keep.tile([2 * ROW_TILES, P], BF16)
-        nc.gpsimd.dma_start(out=vec_rows[:ROW_TILES, :], in_=inv_step.rearrange("(i m) -> i m", m=P))
-        nc.gpsimd.dma_start(out=vec_rows[ROW_TILES:, :], in_=offset.rearrange("(i m) -> i m", m=P))
+        nc.sync.dma_start(out=vec_rows[:ROW_TILES, :], in_=inv_step.rearrange("(i m) -> i m", m=P))
+        nc.sync.dma_start(out=vec_rows[ROW_TILES:, :], in_=offset.rearrange("(i m) -> i m", m=P))
         identity = keep.tile([P, P], F32)
         make_identity(nc, identity[:])
-        vec_square = keep.tile([P, P], F32)
-        nc.gpsimd.memset(vec_square[:], 0.0)
         e_plane = keep.tile([P, PASSES, R], U8, align_bytes=64)
         nc.vector.memset(e_plane[:].bitcast(I32), 0)
+        vec_square = keep.tile([P, P], F32)
+        nc.vector.memset(vec_square[:], 0.0)
 
         load_v(0)
-        load_slab(0, 0, 0)
-        load_slab(0, 1, 1)
-        load_v(1)
         for q in range(4):
             nc.sync.dma_start(
                 out=e_plane[32 * q : 32 * q + 4, :, :].bitcast(I32),
                 in_=e_scales[:, 4 * q : 4 * q + 4, :].rearrange("g r n -> r g n").bitcast(I32),
             )
-        load_slab(0, 2, 2)
-        load_slab(0, 3, 3)
-        load_e(0)
+        load_v(1)
+        load_slab(0, 0)
         load_v(2)
         load_v(3)
+        load_slab(0, 1)
+        load_slab(0, 2)
+        load_e(0)
+        load_slab(0, 3)
+        load_w(0, 0)
         load_e(1)
-        for s in range(len(slabs)):
-            load_slab(1, s, 4 + s)
-        load_w(0, 0, HALF)
-        load_w(0, HALF, HALF)
 
         nc.scalar.activation(out=vec_square[: 2 * ROW_TILES, :], in_=vec_rows[:], func=IDENTITY)
-        turn_v(0)
-        interleave(0, 0)
-        interleave(0, 1)
-        quantize_v(0)
-        quantize_slab(0, 0)
-        turn_v(1)
-        vec_turned = bank(HALF)
+        vec_turned = bank(0)
         nc.tensor.transpose(vec_turned[:, :P], vec_square[:], identity[:])
         by_row = keep.tile([P, 2 * ROW_TILES], F32)
         nc.scalar.copy(out=by_row[:], in_=vec_turned[:, : 2 * ROW_TILES])
-        interleave(0, 2)
-        quantize_slab(0, 1)
+
+        for pair in (0, 1):
+            turn_v(pair)
+            group_v(pair)
+        quantize_v(0)
+        turn_v(2)
+        interleave(0, 0)
         quantize_v(1)
-        interleave(0, 3)
-        quantize_slab(0, 2)
-        quantize_slab(0, 3)
+        interleave(1, 0)
+        quantize_slab(0, 0)
+        group_v(2)
+        quantize_slab(1, 0)
         for n in range(HALF):
             multiply(n, 0)
+        turn_v(3)
+        quantize_v(2)
+        interleave(0, 1)
+        interleave(1, 1)
+        group_v(3)
+        quantize_slab(0, 1)
+        quantize_slab(1, 1)
+        for n in range(HALF):
             multiply(n, 1)
+        for n in range(HALF, ROW_TILES):
+            multiply(n, 0)
+            multiply(n, 1)
+        interleave(0, 2)
+        quantize_v(3)
+        interleave(1, 2)
+        quantize_slab(0, 2)
+        interleave(0, 3)
+        quantize_slab(1, 2)
+        interleave(1, 3)
+        quantize_slab(0, 3)
+        quantize_slab(1, 3)
         for s in (2, 3):
-            for n in range(HALF):
+            for n in range(ROW_TILES):
                 multiply(n, s)
 
-        turn_v(2)
-        turn_v(3)
-        for s in range(len(slabs)):
-            load_slab(2, s, s)
-        load_w(1, 0, ROW_TILES)
-        for s in range(len(slabs)):
-            load_slab(3, s, 8 + s)
-        load_w(2, 0, ROW_TILES)
-        load_w(3, 0, ROW_TILES)
+        load_slab(2, 0)
+        load_w(0, 1)
+        load_slab(2, 1)
+        load_slab(2, 2)
+        load_slab(2, 3)
+        load_w(2, 0)
+        load_w(2, 1)
 
-        interleave(1, 0)
-        quantize_v(2)
-        interleave(1, 1)
-        quantize_v(3)
-        for n in range(HALF, ROW_TILES):
-            multiply_tile(n)
-        quantize_slab(1, 0)
-        interleave(1, 2)
-        quantize_slab(1, 1)
+        def finish_pair(n):
+            for m in (n, n + 1):
+                scale_w(m + 1)
+                finish(m)
+
         scale_w(0)
-        interleave(1, 3)
-        scale_w(1)
-        scale_w(2)
-        quantize_slab(1, 2)
-        finish(0)
-        quantize_slab(1, 3)
-        finish(1)
-
-        for n in range(ROW_TILES, (CHUNKS - 1) * ROW_TILES):
-            j, i = divmod(n, ROW_TILES)
-            multiply_tile(n)
-            if i % 2 == 0:
-                interleave(j + 1, i // 2)
-            scale_w(n - LAG + 1)
-            finish(n - LAG)
-            if i % 2 == 1:
-                quantize_slab(j + 1, i // 2)
-
-        done = (CHUNKS - 1) * ROW_TILES - LAG
+        finish_pair(0)
+        multiply_tile(8)
+        multiply_tile(9)
+        finish_pair(2)
+        multiply_tile(10)
+        multiply_tile(11)
+        interleave(2, 0)
+        finish_pair(4)
+        quantize_slab(2, 0)
+        multiply_tile(12)
+        multiply_tile(13)
+        interleave(3, 0)
+        finish_pair(6)
+        quantize_slab(3, 0)
+        multiply_tile(14)
+        multiply_tile(15)
+        interleave(2, 1)
+        finish_pair(8)
+        quantize_slab(2, 1)
+        interleave(2, 2)
+        finish_pair(10)
+        quantize_slab(2, 2)
+        interleave(2, 3)
+        interleave(3, 1)
+        quantize_slab(2, 3)
+        for s in range(len(slabs)):
+            for n in range(16, 20):
+                multiply(n, s)
+        finish_pair(12)
+        quantize_slab(3, 1)
+        multiply_tile(20)
+        multiply_tile(21)
+        interleave(3, 2)
+        finish_pair(14)
+        quantize_slab(3, 2)
+        multiply_tile(22)
+        multiply_tile(23)
+        interleave(3, 3)
+        finish_pair(16)
+        quantize_slab(3, 3)
+        done = 18
         last = CHUNKS * ROW_TILES
         for n in range((CHUNKS - 1) * ROW_TILES, last):
             multiply_tile(n)

@@ -25,7 +25,8 @@ N_TILE = 512
 ROW_TILES = R // P
 CHUNKS = C // N_TILE
 HALF = ROW_TILES // 2
-VECTOR_COLUMNS = (288, 256)
+VECTOR_COLUMNS = (320, 272)
+AHEAD = 2
 STORES = ((0, 2, (2, 2, 2, 2)), (2, 1, (4, 4)), (3, 1, (4, 2, 1, 1)))
 
 
@@ -44,11 +45,13 @@ def tile_block_error_column_update_e4_kernel(
         v_raw, v_turned, v_grouped, v_mx = {}, {}, {}, {}
         e_codes, w_raw, acc, result = {}, {}, {}, {}
 
-        tiles = [(j, half * HALF + i) for half in range(2) for j in range(2) for i in range(HALF)]
+        tiles = [(d, i + e) for i in range(0, ROW_TILES, 2) for d in range(2) for e in range(2)]
         tiles = tiles + [(j, i) for j in range(2, CHUNKS) for i in range(ROW_TILES)]
+        free_banks = list(range(8))
 
-        def bank(b):
-            return psum.tile([P, N_TILE], F32, name="bank%d" % b)
+        def take_bank():
+            b = free_banks.pop(0)
+            return b, psum.tile([P, N_TILE], F32, name="bank%d" % b)
 
         def load_slab(j, s):
             source, g = slabs[s]
@@ -61,16 +64,13 @@ def tile_block_error_column_update_e4_kernel(
         def load_v(pair):
             raw = keep.tile([P, 2, B], BF16, name="v_raw%d" % pair)
             rows = w_block[pair * 2 * P : (pair + 1) * 2 * P, :]
-            nc.sync.dma_start(out=raw[:], in_=rows.rearrange("(i m) k -> m i k", m=P))
+            nc.sync.dma_start(out=raw[:], in_=rows.rearrange("(m i) k -> m i k", i=2))
             v_raw[pair] = raw
 
-        def load_e(half):
-            width = HALF * P
-            codes = keep.tile([P, PASSES, width], U32, name="e_codes%d" % half, align_bytes=64)
-            words = e_words.rearrange("g p n t -> p g (n t)")
-            words = words[:, :, half * width * PACK : (half + 1) * width * PACK]
-            nc.sync.dma_start(out=codes[:].bitcast(I32), in_=words.bitcast(I32))
-            e_codes[half] = codes
+        def load_e(g):
+            codes = keep.tile([P, R], U32, name="e_codes%d" % g, align_bytes=256)
+            nc.sync.dma_start(out=codes[:].bitcast(I32), in_=e_words[g].rearrange("p n t -> p (n t)").bitcast(I32))
+            e_codes[g] = codes
 
         def load_w(j, half):
             raw = keep.tile([P, HALF, 2 * N_TILE], BF16, name="w%d_%d" % (j, half))
@@ -81,7 +81,7 @@ def tile_block_error_column_update_e4_kernel(
                     w_raw[j + d, half * HALF + i] = raw[:, i, d * N_TILE : (d + 1) * N_TILE]
 
         def interleave(j, s):
-            grouped = stage.tile([P, N_TILE, PACK], BF16, name="grouped", align_bytes=64)
+            grouped = stage.tile([P, N_TILE, PACK], BF16, name="grouped", align_bytes=256)
             split = VECTOR_COLUMNS[j // 2]
             raw = slab_raw[j, s]
             nc.vector.tensor_copy(
@@ -95,8 +95,8 @@ def tile_block_error_column_update_e4_kernel(
             slab_grouped[j, s] = grouped
 
         def quantize(grouped, name):
-            codes = keep.tile([P, N_TILE], U32, name="codes_" + name, align_bytes=64)
-            scales = keep.tile([P, N_TILE], U8, name="scales_" + name, align_bytes=64)
+            codes = keep.tile([P, N_TILE], U32, name="codes_" + name, align_bytes=256)
+            scales = keep.tile([P, N_TILE], U8, name="scales_" + name, align_bytes=256)
             nc.vector.quantize_mx(out=codes[:].bitcast(E4M3X4), scales=scales[:], in_=grouped)
             return codes, scales
 
@@ -107,42 +107,43 @@ def tile_block_error_column_update_e4_kernel(
             v_mx[pair] = quantize(v_grouped[pair][:], "v%d" % pair)
 
         def turn_v(pair):
-            for i in range(2):
-                words = v_raw[pair][:, i, :].bitcast(F32)
-                turned = bank(HALF + (2 * pair + i) % HALF)
-                for g in range(PASSES):
+            for g in range(PASSES):
+                b, turned = take_bank()
+                for i in range(2):
+                    words = v_raw[pair][:, i, :].bitcast(F32)
                     for u in range(2):
-                        slot = (2 * g + u) * P
+                        slot = (2 * i + u) * P
                         nc.tensor.transpose(
                             turned[:, slot : slot + P], words[:, 2 * P * g + u : 2 * P * (g + 1) : 2], identity[:]
                         )
-                v_turned[2 * pair + i] = turned
+                v_turned[pair, g] = b, turned
 
         def group_v(pair):
-            grouped = stage.tile([P, N_TILE * PACK], BF16, name="grouped", align_bytes=64)
-            for i in range(2):
-                turned = v_turned[2 * pair + i]
+            grouped = stage.tile([P, N_TILE * PACK], BF16, name="grouped", align_bytes=256)
+            for g in range(PASSES):
+                b, turned = v_turned[pair, g]
                 nc.scalar.copy(
-                    out=grouped[:, i * B : (i + 1) * B].bitcast(F32).rearrange("p (g m u) -> p g m u", g=PASSES, u=2),
-                    in_=turned[:].rearrange("p (g u m) -> p g m u", g=PASSES, u=2),
+                    out=grouped[:, g * B : (g + 1) * B].bitcast(F32).rearrange("p (m i u) -> p m i u", i=2, u=2),
+                    in_=turned[:].rearrange("p (i u m) -> p m i u", i=2, u=2),
                 )
+                free_banks.append(b)
             v_grouped[pair] = grouped
 
         def multiply(n, s):
             j, i = tiles[n]
             g = slabs[s][1]
             if s == 0:
-                acc[n] = bank(n % ROW_TILES)
+                acc[n] = take_bank()
             if s < PASSES:
                 codes, scales = v_mx[i // 2]
-                cols = slice((i % 2 * PASSES + g) * P, (i % 2 * PASSES + g + 1) * P)
+                cols = slice((2 * g + i % 2) * P, (2 * g + i % 2 + 1) * P)
                 lhs, lhs_scale = codes[:, cols].bitcast(E4M3X4), scales[:, cols]
             else:
-                lhs = e_codes[i // HALF][:, g, i % HALF * P : (i % HALF + 1) * P].bitcast(E5M2X4)
+                lhs = e_codes[g][:, i * P : (i + 1) * P].bitcast(E5M2X4)
                 lhs_scale = e_plane[:, g, i * P : (i + 1) * P]
             rhs_codes, rhs_scales = slab_mx[j, s]
             nc.tensor.matmul_mx(
-                out=acc[n][:],
+                out=acc[n][1][:],
                 lhsT=lhs,
                 lhsT_scale=lhs_scale,
                 rhs=rhs_codes[:].bitcast(E4M3X4),
@@ -181,25 +182,26 @@ def tile_block_error_column_update_e4_kernel(
             i = tiles[n][1]
             target = result[tiles[n]]
             nc.vector.scalar_tensor_tensor(
-                out=target, in0=acc[n][:], scalar=by_row[:, i : i + 1], in1=target, op0=MULT, op1=ADD
+                out=target, in0=acc[n][1][:], scalar=by_row[:, i : i + 1], in1=target, op0=MULT, op1=ADD
             )
+            free_banks.append(acc[n][0])
             if tiles[n] in runs:
                 staged, rows = runs[tiles[n]]
                 nc.sync.dma_start(out=rows.rearrange("(i m) c -> m i c", m=P), in_=staged[:])
 
         vec_rows = keep.tile([2 * ROW_TILES, P], BF16)
-        nc.sync.dma_start(out=vec_rows[:ROW_TILES, :], in_=inv_step.rearrange("(i m) -> i m", m=P))
-        nc.sync.dma_start(out=vec_rows[ROW_TILES:, :], in_=offset.rearrange("(i m) -> i m", m=P))
+        nc.scalar.dma_start(out=vec_rows[:ROW_TILES, :], in_=inv_step.rearrange("(i m) -> i m", m=P))
+        nc.scalar.dma_start(out=vec_rows[ROW_TILES:, :], in_=offset.rearrange("(i m) -> i m", m=P))
         identity = keep.tile([P, P], F32)
         make_identity(nc, identity[:])
-        e_plane = keep.tile([P, PASSES, R], U8, align_bytes=64)
+        e_plane = keep.tile([P, PASSES, R], U8, align_bytes=256)
         nc.vector.memset(e_plane[:].bitcast(I32), 0)
         vec_square = keep.tile([P, P], F32)
         nc.vector.memset(vec_square[:], 0.0)
 
         load_v(0)
         for q in range(4):
-            nc.sync.dma_start(
+            nc.gpsimd.dma_start(
                 out=e_plane[32 * q : 32 * q + 4, :, :].bitcast(I32),
                 in_=e_scales[:, 4 * q : 4 * q + 4, :].rearrange("g r n -> r g n").bitcast(I32),
             )
@@ -211,15 +213,17 @@ def tile_block_error_column_update_e4_kernel(
         load_slab(0, 2)
         load_e(0)
         load_slab(0, 3)
-        load_w(0, 0)
         load_e(1)
+        load_w(0, 0)
 
         nc.scalar.activation(out=vec_square[: 2 * ROW_TILES, :], in_=vec_rows[:], func=IDENTITY)
-        vec_turned = bank(0)
+        vec_bank, vec_turned = take_bank()
         nc.tensor.transpose(vec_turned[:, :P], vec_square[:], identity[:])
         by_row = keep.tile([P, 2 * ROW_TILES], F32)
         nc.scalar.copy(out=by_row[:], in_=vec_turned[:, : 2 * ROW_TILES])
+        free_banks.append(vec_bank)
 
+        lower, upper = (0, 1, 4, 5), (2, 3, 6, 7)
         for pair in (0, 1):
             turn_v(pair)
             group_v(pair)
@@ -231,7 +235,7 @@ def tile_block_error_column_update_e4_kernel(
         quantize_slab(0, 0)
         group_v(2)
         quantize_slab(1, 0)
-        for n in range(HALF):
+        for n in lower:
             multiply(n, 0)
         turn_v(3)
         quantize_v(2)
@@ -240,9 +244,9 @@ def tile_block_error_column_update_e4_kernel(
         group_v(3)
         quantize_slab(0, 1)
         quantize_slab(1, 1)
-        for n in range(HALF):
+        for n in lower:
             multiply(n, 1)
-        for n in range(HALF, ROW_TILES):
+        for n in upper:
             multiply(n, 0)
             multiply(n, 1)
         interleave(0, 2)
@@ -255,7 +259,7 @@ def tile_block_error_column_update_e4_kernel(
         quantize_slab(0, 3)
         quantize_slab(1, 3)
         for s in (2, 3):
-            for n in range(ROW_TILES):
+            for n in lower + upper:
                 multiply(n, s)
 
         load_slab(2, 0)
@@ -268,10 +272,11 @@ def tile_block_error_column_update_e4_kernel(
 
         def finish_pair(n):
             for m in (n, n + 1):
-                scale_w(m + 1)
+                scale_w(m + AHEAD)
                 finish(m)
 
-        scale_w(0)
+        for m in range(AHEAD):
+            scale_w(m)
         finish_pair(0)
         multiply_tile(8)
         multiply_tile(9)
@@ -318,7 +323,7 @@ def tile_block_error_column_update_e4_kernel(
             multiply_tile(n)
             upto = min(done + 2, n + 1)
             for m in range(done, upto):
-                if m + 1 < last:
-                    scale_w(m + 1)
+                if m + AHEAD < last:
+                    scale_w(m + AHEAD)
                 finish(m)
             done = upto

@@ -25,8 +25,9 @@ N_TILE = 512
 ROW_TILES = R // P
 CHUNKS = C // N_TILE
 HALF = ROW_TILES // 2
-VECTOR_COLUMNS = (320, 272)
+VECTOR_COLUMNS = (320, 288)
 AHEAD = 2
+SCALAR_STORES = ((2, 7), (3, 5), (3, 7))
 STORES = ((0, 2, (2, 2, 2, 2)), (2, 1, (4, 4)), (3, 1, (4, 2, 1, 1)))
 
 
@@ -187,7 +188,8 @@ def tile_block_error_column_update_e4_kernel(
             free_banks.append(acc[n][0])
             if tiles[n] in runs:
                 staged, rows = runs[tiles[n]]
-                nc.sync.dma_start(out=rows.rearrange("(i m) c -> m i c", m=P), in_=staged[:])
+                queue = nc.scalar if tiles[n] in SCALAR_STORES else nc.sync
+                queue.dma_start(out=rows.rearrange("(i m) c -> m i c", m=P), in_=staged[:])
 
         vec_rows = keep.tile([2 * ROW_TILES, P], BF16)
         nc.scalar.dma_start(out=vec_rows[:ROW_TILES, :], in_=inv_step.rearrange("(i m) -> i m", m=P))

from contextlib import ExitStack

import concourse.mybir as mybir
from concourse.masks import make_identity

R, B, C = 1024, 1024, 2048
FLOPS = 2 * 2 * R * B * C

F32 = mybir.dt.float32
BF16 = mybir.dt.bfloat16
I32 = mybir.dt.int32
U32 = mybir.dt.uint32
U8 = mybir.dt.uint8
E4M3X4 = mybir.dt.float8_e4m3fn_x4
E5M2X4 = mybir.dt.float8_e5m2_x4
IDENTITY = mybir.ActivationFunctionType.Identity
MULT = mybir.AluOpType.mult
ADD = mybir.AluOpType.add

P = 128
PACK = 4
K_PASS = P * PACK
PASSES = B // K_PASS
N_TILE = 512
ROW_TILES = R // P
CHUNKS = C // N_TILE
HALF = ROW_TILES // 2
VECTOR_COLUMNS = (320, 288)
AHEAD = 2
SCALAR_STORES = ((2, 7), (3, 5), (3, 7))
STORES = ((0, 2, (2, 2, 2, 2)), (2, 1, (4, 4)), (3, 1, (4, 2, 1, 1)))


def tile_block_error_column_update_e4_kernel(
    tc, e_words, e_scales, u_rows, w_block, asym_rows, w_rest, inv_step, offset, out
):
    nc = tc.nc
    with ExitStack() as ctx:
        keep = ctx.enter_context(tc.tile_pool(name="keep", bufs=1))
        stage = ctx.enter_context(tc.tile_pool(name="stage", bufs=5))
        psum = ctx.enter_context(tc.psum_pool(name="psum", bufs=1))
        ctx.enter_context(tc.manual_schedule())

        slabs = [(asym_rows, 0), (asym_rows, 1), (u_rows, 0), (u_rows, 1)]
        slab_raw, slab_grouped, slab_mx = {}, {}, {}
        v_raw, v_turned, v_grouped, v_mx = {}, {}, {}, {}
        e_codes, w_raw, acc, result = {}, {}, {}, {}

        tiles = [(d, i + e) for i in range(0, ROW_TILES, 2) for d in range(2) for e in range(2)]
        tiles = tiles + [(j, i) for j in range(2, CHUNKS) for i in range(ROW_TILES)]
        free_banks = list(range(8))

        def take_bank():
            b = free_banks.pop(0)
            return b, psum.tile([P, N_TILE], F32, name="bank%d" % b)

        def load_slab(j, s):
            source, g = slabs[s]
            raw = keep.tile([P, PACK, 2 * N_TILE], BF16, name="raw%d" % s)
            rows = source[g * K_PASS : (g + 1) * K_PASS, j * N_TILE : (j + 2) * N_TILE]
            nc.sync.dma_start(out=raw[:], in_=rows.rearrange("(p t) c -> p t c", t=PACK))
            for d in range(2):
                slab_raw[j + d, s] = raw[:, :, d * N_TILE : (d + 1) * N_TILE]

        def load_v(pair):
            raw = keep.tile([P, 2, B], BF16, name="v_raw%d" % pair)
            rows = w_block[pair * 2 * P : (pair + 1) * 2 * P, :]
            nc.sync.dma_start(out=raw[:], in_=rows.rearrange("(m i) k -> m i k", i=2))
            v_raw[pair] = raw

        def load_e(g):
            codes = keep.tile([P, R], U32, name="e_codes%d" % g, align_bytes=256)
            nc.sync.dma_start(out=codes[:].bitcast(I32), in_=e_words[g].rearrange("p n t -> p (n t)").bitcast(I32))
            e_codes[g] = codes

        def load_w(j, half):
            raw = keep.tile([P, HALF, 2 * N_TILE], BF16, name="w%d_%d" % (j, half))
            rows = w_rest[half * HALF * P : (half + 1) * HALF * P, j * N_TILE : (j + 2) * N_TILE]
            nc.sync.dma_start(out=raw[:], in_=rows.rearrange("(i m) c -> m i c", m=P))
            for i in range(HALF):
                for d in range(2):
                    w_raw[j + d, half * HALF + i] = raw[:, i, d * N_TILE : (d + 1) * N_TILE]

        def interleave(j, s):
            grouped = stage.tile([P, N_TILE, PACK], BF16, name="grouped", align_bytes=256)
            split = VECTOR_COLUMNS[j // 2]
            raw = slab_raw[j, s]
            nc.vector.tensor_copy(
                out=grouped[:, :split, :].rearrange("p (c i) t -> p c t i", i=4),
                in_=raw[:, :, :split].rearrange("p t (c i) -> p c t i", i=4),
            )
            nc.scalar.copy(
                out=grouped[:, split:, :].rearrange("p (c i) t -> p c t i", i=4),
                in_=raw[:, :, split:].rearrange("p t (c i) -> p c t i", i=4),
            )
            slab_grouped[j, s] = grouped

        def quantize(grouped, name):
            codes = keep.tile([P, N_TILE], U32, name="codes_" + name, align_bytes=256)
            scales = keep.tile([P, N_TILE], U8, name="scales_" + name, align_bytes=256)
            nc.vector.quantize_mx(out=codes[:].bitcast(E4M3X4), scales=scales[:], in_=grouped)
            return codes, scales

        def quantize_slab(j, s):
            slab_mx[j, s] = quantize(slab_grouped[j, s][:].rearrange("p c t -> p (c t)"), "%d_%d" % (j, s))

        def quantize_v(pair):
            v_mx[pair] = quantize(v_grouped[pair][:], "v%d" % pair)

        def turn_v(pair):
            for g in range(PASSES):
                b, turned = take_bank()
                for i in range(2):
                    words = v_raw[pair][:, i, :].bitcast(F32)
                    for u in range(2):
                        slot = (2 * i + u) * P
                        nc.tensor.transpose(
                            turned[:, slot : slot + P], words[:, 2 * P * g + u : 2 * P * (g + 1) : 2], identity[:]
                        )
                v_turned[pair, g] = b, turned

        def group_v(pair):
            grouped = stage.tile([P, N_TILE * PACK], BF16, name="grouped", align_bytes=256)
            for g in range(PASSES):
                b, turned = v_turned[pair, g]
                nc.scalar.copy(
                    out=grouped[:, g * B : (g + 1) * B].bitcast(F32).rearrange("p (m i u) -> p m i u", i=2, u=2),
                    in_=turned[:].rearrange("p (i u m) -> p m i u", i=2, u=2),
                )
                free_banks.append(b)
            v_grouped[pair] = grouped

        def multiply(n, s):
            j, i = tiles[n]
            g = slabs[s][1]
            if s == 0:
                acc[n] = take_bank()
            if s < PASSES:
                codes, scales = v_mx[i // 2]
                cols = slice((2 * g + i % 2) * P, (2 * g + i % 2 + 1) * P)
                lhs, lhs_scale = codes[:, cols].bitcast(E4M3X4), scales[:, cols]
            else:
                lhs = e_codes[g][:, i * P : (i + 1) * P].bitcast(E5M2X4)
                lhs_scale = e_plane[:, g, i * P : (i + 1) * P]
            rhs_codes, rhs_scales = slab_mx[j, s]
            nc.tensor.matmul_mx(
                out=acc[n][1][:],
                lhsT=lhs,
                lhsT_scale=lhs_scale,
                rhs=rhs_codes[:].bitcast(E4M3X4),
                rhs_scale=rhs_scales[:],
                start=(s == 0),
                stop=(s == len(slabs) - 1),
            )

        def multiply_tile(n):
            for s in range(len(slabs)):
                multiply(n, s)

        runs = {}
        for j, span, counts in STORES:
            first = 0
            for count in counts:
                staged = keep.tile([P, count, span * N_TILE], F32, name="out%d_%d" % (j, first))
                for i in range(count):
                    for d in range(span):
                        result[j + d, first + i] = staged[:, i, d * N_TILE : (d + 1) * N_TILE]
                rows = out[first * P : (first + count) * P, j * N_TILE : (j + span) * N_TILE]
                runs[j + span - 1, first + count - 1] = (staged, rows)
                first = first + count

        def scale_w(n):
            i = tiles[n][1]
            nc.scalar.activation(
                out=result[tiles[n]],
                in_=w_raw[tiles[n]],
                func=IDENTITY,
                scale=by_row[:, i : i + 1],
                bias=by_row[:, ROW_TILES + i : ROW_TILES + i + 1],
            )

        def finish(n):
            i = tiles[n][1]
            target = result[tiles[n]]
            nc.vector.scalar_tensor_tensor(
                out=target, in0=acc[n][1][:], scalar=by_row[:, i : i + 1], in1=target, op0=MULT, op1=ADD
            )
            free_banks.append(acc[n][0])
            if tiles[n] in runs:
                staged, rows = runs[tiles[n]]
                queue = nc.scalar if tiles[n] in SCALAR_STORES else nc.sync
                queue.dma_start(out=rows.rearrange("(i m) c -> m i c", m=P), in_=staged[:])

        vec_rows = keep.tile([2 * ROW_TILES, P], BF16)
        nc.scalar.dma_start(out=vec_rows[:ROW_TILES, :], in_=inv_step.rearrange("(i m) -> i m", m=P))
        nc.scalar.dma_start(out=vec_rows[ROW_TILES:, :], in_=offset.rearrange("(i m) -> i m", m=P))
        identity = keep.tile([P, P], F32)
        make_identity(nc, identity[:])
        e_plane = keep.tile([P, PASSES, R], U8, align_bytes=256)
        nc.vector.memset(e_plane[:].bitcast(I32), 0)
        vec_square = keep.tile([P, P], F32)
        nc.vector.memset(vec_square[:], 0.0)

        load_v(0)
        for q in range(4):
            nc.gpsimd.dma_start(
                out=e_plane[32 * q : 32 * q + 4, :, :].bitcast(I32),
                in_=e_scales[:, 4 * q : 4 * q + 4, :].rearrange("g r n -> r g n").bitcast(I32),
            )
        load_v(1)
        load_slab(0, 0)
        load_v(2)
        load_v(3)
        load_slab(0, 1)
        load_slab(0, 2)
        load_e(0)
        load_slab(0, 3)
        load_e(1)
        load_w(0, 0)

        nc.scalar.activation(out=vec_square[: 2 * ROW_TILES, :], in_=vec_rows[:], func=IDENTITY)
        vec_bank, vec_turned = take_bank()
        nc.tensor.transpose(vec_turned[:, :P], vec_square[:], identity[:])
        by_row = keep.tile([P, 2 * ROW_TILES], F32)
        nc.scalar.copy(out=by_row[:], in_=vec_turned[:, : 2 * ROW_TILES])
        free_banks.append(vec_bank)

        lower, upper = (0, 1, 4, 5), (2, 3, 6, 7)
        for pair in (0, 1):
            turn_v(pair)
            group_v(pair)
        quantize_v(0)
        turn_v(2)
        interleave(0, 0)
        quantize_v(1)
        interleave(1, 0)
        quantize_slab(0, 0)
        group_v(2)
        quantize_slab(1, 0)
        for n in lower:
            multiply(n, 0)
        turn_v(3)
        quantize_v(2)
        interleave(0, 1)
        interleave(1, 1)
        group_v(3)
        quantize_slab(0, 1)
        quantize_slab(1, 1)
        for n in lower:
            multiply(n, 1)
        for n in upper:
            multiply(n, 0)
            multiply(n, 1)
        interleave(0, 2)
        quantize_v(3)
        interleave(1, 2)
        quantize_slab(0, 2)
        interleave(0, 3)
        quantize_slab(1, 2)
        interleave(1, 3)
        quantize_slab(0, 3)
        quantize_slab(1, 3)
        for s in (2, 3):
            for n in lower + upper:
                multiply(n, s)

        load_slab(2, 0)
        load_w(0, 1)
        load_slab(2, 1)
        load_slab(2, 2)
        load_slab(2, 3)
        load_w(2, 0)
        load_w(2, 1)

        def finish_pair(n):
            for m in (n, n + 1):
                scale_w(m + AHEAD)
                finish(m)

        for m in range(AHEAD):
            scale_w(m)
        finish_pair(0)
        multiply_tile(8)
        multiply_tile(9)
        finish_pair(2)
        multiply_tile(10)
        multiply_tile(11)
        interleave(2, 0)
        finish_pair(4)
        quantize_slab(2, 0)
        multiply_tile(12)
        multiply_tile(13)
        interleave(3, 0)
        finish_pair(6)
        quantize_slab(3, 0)
        multiply_tile(14)
        multiply_tile(15)
        interleave(2, 1)
        finish_pair(8)
        quantize_slab(2, 1)
        interleave(2, 2)
        finish_pair(10)
        quantize_slab(2, 2)
        interleave(2, 3)
        interleave(3, 1)
        quantize_slab(2, 3)
        for s in range(len(slabs)):
            for n in range(16, 20):
                multiply(n, s)
        finish_pair(12)
        quantize_slab(3, 1)
        multiply_tile(20)
        multiply_tile(21)
        interleave(3, 2)
        finish_pair(14)
        quantize_slab(3, 2)
        multiply_tile(22)
        multiply_tile(23)
        interleave(3, 3)
        finish_pair(16)
        quantize_slab(3, 3)
        done = 18
        last = CHUNKS * ROW_TILES
        for n in range((CHUNKS - 1) * ROW_TILES, last):
            multiply_tile(n)
            upto = min(done + 2, n + 1)
            for m in range(done, upto):
                if m + AHEAD < last:
                    scale_w(m + AHEAD)
                finish(m)
            done = upto
